import numpy as np, ml_dtypes
CORES = [48,51,52,55]
N = 4
BF = ml_dtypes.bfloat16
def gentries(a):
    return np.ascontiguousarray(a.reshape(8, 16, -1).transpose(0, 2, 1)).reshape(8, -1)
def gtable(e):
    e = np.asarray(e); return np.ascontiguousarray(e.reshape(8, -1, 16).transpose(0, 2, 1)).reshape(128, -1).astype(np.int32)
S, CAP, H = 4096, 1120, 2
def channel(rng):
    v = rng.integers(-45, 46, (N, 128, S)) + rng.integers(-24, -4, (N, 128, 1))
    return np.clip(v, -63, 63).astype(np.float32).astype(BF)
def counts(rng):
    n = np.full((N, N), S // N, np.int64)
    for i in range(4 * N):
        q = rng.choice(N, 2, replace=False); r = rng.choice(N, 2, replace=False)
        d = min(CAP - n[q[0], r[0]], CAP - n[q[1], r[1]], n[q[0], r[1]], n[q[1], r[0]], (CAP - S // N) // 3 + 1)
        d = rng.integers(0, d + 1); n[q[0], r[0]] += d; n[q[1], r[1]] += d; n[q[0], r[1]] -= d; n[q[1], r[0]] -= d
    return n
def slots(rng, n, runs=False):
    sa = np.zeros((N, 8, S), np.int32); sb = np.zeros((N, 8, S), np.int32)
    def places():
        return rng.permutation(S) if not runs else np.arange(S) if rng.integers(0, 2) else np.arange(S)[::-1]
    for g in range(8):
        pa = [places() for q in range(N)]; pb = [places() for r in range(N)]
        for q in range(N):
            for r in range(N):
                m = int(n[g][q, r]); i = int(np.sum(n[g][q, :r])); j = int(np.sum(n[g][:q, r]))
                c = np.arange(m) if runs else rng.permutation(CAP)[:m]
                sa[q, g, pa[q][i:i + m]] = r * CAP + c; sb[r, g, pb[r][j:j + m]] = q * CAP + c
    return {"sa": np.stack([gtable(v) for v in sa]), "sb": np.stack([gtable(v) for v in sb])}
def setup_inputs(rng):
    d = {"a": channel(rng), "b": channel(rng)}
    d.update(slots(rng, [counts(rng) for g in range(8)])); return d
def setup_inputs_full(rng):
    d = setup_inputs(rng); n = np.full((8, N, N), S // N, np.int64); q = np.arange(N)
    for g in range(8):
        k = rng.integers(1, N); l = (k + rng.integers(1, N)) % N
        n[g, q, (q + k) % N] += CAP - S // N; n[g, q, (q + l) % N] -= CAP - S // N
    d.update(slots(rng, n)); return d
def setup_inputs_runs(rng):
    d = setup_inputs(rng); d.update(slots(rng, [counts(rng) for g in range(8)], True)); return d
def setup_inputs_ends(rng):
    d = setup_inputs(rng); vals = np.array([-63, -63, -63, -63, -15, -1, 0, 1, 15, 63]); k = rng.permutation(128)
    for name in ("a", "b"):
        v = rng.choice(vals, (N, 128, S)); v[:, k[:64]] = np.repeat(rng.choice(vals, (N, 64, S // 32)), 32, axis=2)
        v[:, k[0]] = 63; v[:, k[1]] = -63; v[:, k[2]] = 0
        d[name] = v.astype(np.float32).astype(BF)
    return d
def setup_inputs_spread(rng):
    d = setup_inputs(rng)
    for name in ("a", "b"):
        amp = 2 ** rng.integers(0, 7, (N, 1, S)) - 1
        v = np.minimum(np.floor(rng.random((N, 128, S)) ** 3 * (2 * amp + 1)), 2 * amp) - amp
        d[name] = v.astype(np.float32).astype(BF)
    return d
def check_inputs(d):
    bad = []
    try:
        for k in ("a", "b"):
            v = np.asarray(d[k]).astype(np.float64)
            if v.shape != (N, 128, S) or not np.isfinite(v).all() or (v != np.floor(v)).any() or (np.abs(v) > 63).any(): bad.append(k)
        used = []
        for k in ("sa", "sb"):
            v = np.asarray(d[k])
            if v.shape != (N, 128, S // 16) or v.min() < 0 or v.max() >= N * CAP:
                bad.append(k); continue
            u = np.zeros((N, 8, N * CAP), bool)
            for r in range(N): u[r][np.arange(8)[:, None], gentries(v[r])] = True
            if (np.sum(u, axis=-1) != S).any(): bad.append(k + " repeats")
            used.append(u.reshape(N, 8, N, CAP))
        if len(used) == 2 and (used[0] != used[1].transpose(2, 1, 0, 3)).any(): bad.append("slots of pairs")
    except Exception:
        bad.append("inputs")
    return bad
def partners(sa, sb):
    g = np.arange(8)[:, None]; inv = np.zeros((N, 8, N * CAP), np.int64); src = np.zeros((8, N * S), np.int64)
    for q in range(N): inv[q][g, gentries(sa[q])] = np.arange(S)
    for r in range(N):
        s = gentries(sb[r]).astype(np.int64); q = s // CAP
        src[:, r * S:(r + 1) * S] = q * S + inv[q, g, r * CAP + s - q * CAP]
    return src
def carry(e, src, back):
    x = np.ascontiguousarray(e.reshape(N, 8, 16, S).transpose(1, 2, 0, 3)).reshape(8, 16, N * S); z = np.zeros_like(x)
    for g in range(8):
        if back: z[g][:, src[g]] = x[g]
        else: z[g] = x[g][:, src[g]]
    return np.ascontiguousarray(z.reshape(8, 16, N, S).transpose(2, 0, 1, 3)).reshape(N, 128, S)
def scan(v, back):
    x = np.ascontiguousarray(np.moveaxis(v, -1, 0)); z = np.zeros_like(x); s = np.zeros_like(x[0])
    for t in (range(S - 1, -1, -1) if back else range(S)):
        s = np.maximum(s + x[t], 0); z[t] = s
    return np.moveaxis(z, 0, -1)
def extrinsic(v):
    e = np.full(v.shape, -15, np.int64)
    e[..., 1:] += np.minimum(scan(v, False), 15)[..., :-1]
    e[..., :-1] += np.minimum(scan(v, True), 15)[..., 1:]
    return e
def reference(a, b, sa, sb):
    src = partners(sa, sb)
    ca = a.astype(np.float32).astype(np.int64); cb = b.astype(np.float32).astype(np.int64)
    prior = np.zeros((N, 128, S), np.int64)
    for h in range(H // 2):
        prior = carry(extrinsic(ca + prior), src, False)
        prior = carry(extrinsic(cb + prior), src, True)
    return {"y": (ca + prior).astype(np.float32).astype(BF)}

@@ -1,0 +1,269 @@
+from concourse.bass import DstId, RemoteDMATransfer
+from concourse.mybir import AluOpType, ActivationFunctionType as AF
+
+S, CAP, N = 4096, 1120, 4
+W = N * CAP
+K = W // 16
+KB = CAP // 16
+KS = S // 16
+OFS = 64
+C1 = 1024
+XF = W // 2
+P1, P2 = 1152, 2624
+NS, CS = 3, 448
+VS = S - NS * CS
+NQ, CQ = 4, 448
+VQ = S - NQ * CQ
+VCUT = (0, 768, 1536, VQ)
+VB = 608
+BF, F32, I32, U16 = "bfloat16", "float32", "int32", "uint16"
+
+SCRATCH = {
+    "av": ("sbuf", [128, S], BF), "bv": ("sbuf", [128, S], BF), "bq": ("sbuf", [128, VS], BF),
+    "cst": ("sbuf", [128, S], BF),
+    "fx": ("sbuf", [128, C1 + 16], F32),
+    "fw": ("sbuf", [128, S + 16], BF),
+    "bw": ("sbuf", [128, S + 16], BF),
+    "fc": ("sbuf", [128, S], BF), "bc": ("sbuf", [128, S], BF),
+    "xs": ("sbuf", [128, W], BF), "ys": ("sbuf", [128, W], BF),
+    "gs": ("sbuf", [128, NS * CS], BF), "ln": ("sbuf", [128, S], BF),
+    "gf": ("sbuf", [128, W], BF), "gb": ("sbuf", [128, W], BF), "y2": ("sbuf", [128, W], BF),
+    "vt": ("sbuf", [128, VQ], BF), "ge": ("sbuf", [128, NQ * CQ], BF), "qv": ("sbuf", [128, S], BF),
+    "sai": ("sbuf", [128, KS], I32), "sbi": ("sbuf", [128, KS], I32),
+    "t1": ("sbuf", [128, KS], I32), "t3": ("sbuf", [128, KS], I32), "t4": ("sbuf", [128, KS], I32),
+    "sau": ("sbuf", [128, KS], U16), "sbu": ("sbuf", [128, KS], U16), "sbp": ("sbuf", [128, KS], U16),
+    "plc": ("sbuf", [128, S], F32), "inv": ("sbuf", [128, W], F32),
+    "tab": ("sbuf", [128, K], F32), "invu": ("sbuf", [128, K], U16),
+    "onp": ("sbuf", [128, 128], BF), "onm": ("sbuf", [128, 128], BF),
+    "idp": ("sbuf", [128, 128], BF), "idm": ("sbuf", [128, 128], BF),
+}
+for _k in range(8):
+    SCRATCH["ps%d" % _k] = ("psum", [128, 512], F32)
+SEMAPHORES = ["lda1", "lda2", "ldsa", "ldsb", "ldb", "z1", "z2", "zx0", "zf", "zb", "zxs", "zxd", "l1", "l3", "l4",
+              "lsb", "lsbp", "lsa", "iot", "ifl", "ones", "idt", "f1a", "f1b", "b1", "fa", "fb", "fd", "bc0", "bc1", "bc2",
+              "x0", "x1", "x2", "own1", "arr1", "loc1", "bq", "inv", "tab", "invu", "ln", "f2", "b2",
+              "gf0", "gf1", "gf2", "gf3", "gb0", "gb1", "gb2", "gb3", "gc0", "gc3", "pown", "own2", "own3", "arr2",
+              "loc2", "acc"]
+SEMAPHORES += ["%s%d" % (n, k) for n in ("gs", "pl", "lc", "ge", "pq", "qs") for k in range(4)]
+SEMAPHORES += ["%s%d" % (n, k) for n in ("vt", "qv") for k in range(3)]
+
+
+def rank_program(g, core, T, topo):
+    q = T.rank_of(core)
+    if q is None:
+        return
+    v, s, sy, te, sem = g.vector, g.scalar, g.sync, g.tensor, T.sem
+    A = AluOpType
+    others = [r for r in range(N) if r != q]
+    others.sort(key=lambda r: (topo.die(T.cores[r]) == topo.die(core), (r - q) % N))
+    order = others + [q]
+
+    def blk(r, lo=0, hi=CAP):
+        return slice(r * CAP + lo, r * CAP + hi)
+
+    def lst(r, lo=0, hi=CAP):
+        return T.invu[:, r * KB + lo // 16:r * KB + hi // 16]
+
+    def dst(r):
+        rid, pid, _ = topo.addr(T.cores[r])
+        return DstId(rid=rid, pnc=pid)
+
+    sy.dma_start(T.av[:, 0:C1], T.a[:, 0:C1]).then_inc(sem.lda1, 16)
+    sy.dma_start(T.sbi[:], T.sb[:]).then_inc(sem.ldsb, 16)
+    sy.dma_start(T.av[:, C1:S], T.a[:, C1:S]).then_inc(sem.lda2, 16)
+    sy.dma_start(T.sai[:], T.sa[:]).then_inc(sem.ldsa, 16)
+    sy.dma_start(T.xs[:, XF:W], T.b[:, 0:W - XF]).then_inc(sem.zxd, 16)
+    sy.dma_start(T.bv[:], T.b[:]).then_inc(sem.ldb, 16)
+    sy.wait_ge(sem.inv, 1)
+    sy.dma_start(T.tab[:], T.inv[0:128:16, :]).then_inc(sem.tab, 16)
+
+    g.dma_start(T.inv[0:128:16, 0:S], T.a[0:8, :]).then_inc(sem.ifl, 16)
+    g.dma_start(T.inv[0:128:16, S:W], T.a[0:8, 0:W - S]).then_inc(sem.ifl, 16)
+    g.iota(T.plc[:], [[1, S]], OFS, 0, allow_small_or_imprecise_dtypes=True).then_inc(sem.iot, 1)
+    g.iota(T.onp[:], [[0, 128]], 1, 0, allow_small_or_imprecise_dtypes=True).then_inc(sem.ones, 1)
+    g.iota(T.onm[:], [[0, 128]], -1, 0, allow_small_or_imprecise_dtypes=True).then_inc(sem.ones, 1)
+    g.wait_ge(sem.ones, 2)
+    g.affine_select(T.idp[:], T.onp[:], [[-1, 128]], A.is_equal, 0.0, 0, 1).then_inc(sem.idt, 1)
+    g.affine_select(T.idm[:], T.onm[:], [[-1, 128]], A.is_equal, 0.0, 0, 1).then_inc(sem.idt, 1)
+
+    v.memset(T.cst[:, 0:CAP], -15.0).then_inc(sem.z1, 1)
+    v.memset(T.fx[:, 0:1], -15.0).then_inc(sem.zx0, 1)
+    v.memset(T.cst[:, CAP:S], -15.0).then_inc(sem.z2, 1)
+    v.memset(T.fw[:, 0:1], -15.0).then_inc(sem.zf, 1)
+    v.memset(T.bw[:, S + 15:S + 16], -15.0).then_inc(sem.zb, 1)
+    v.wait_ge(sem.z1, 1)
+    v.wait_ge(sem.lda1, 16)
+    v.tensor_tensor_scan(T.fx[:, 1:C1 + 1], T.av[:, 0:C1], T.cst[:, 0:C1], -15.0, A.add, A.max).then_inc(sem.f1a, 1)
+    v.wait_ge(sem.ldsb, 16)
+    v.tensor_scalar(T.t1[:], T.sbi[:], 15, None, A.bitwise_and).then_inc(sem.l1, 1)
+    v.tensor_copy(T.sbu[:], T.sbi[:]).then_inc(sem.lsb, 1)
+    v.wait_ge(sem.l1, 1)
+    v.tensor_scalar(T.t3[:], T.t1[:], 16 * K - 1, None, A.mult).then_inc(sem.l3, 1)
+    v.wait_ge(sem.l3, 1)
+    v.tensor_tensor(T.t4[:], T.t3[:], T.sbi[:], A.add).then_inc(sem.l4, 1)
+    v.wait_ge(sem.l4, 1)
+    v.tensor_scalar(T.sbp[:], T.t4[:], 0.0625, None, A.mult).then_inc(sem.lsbp, 1)
+    v.wait_ge(sem.z2, 1)
+    v.wait_ge(sem.f1a, 1)
+    v.wait_ge(sem.lda2, 16)
+    v.tensor_tensor_scan(T.fw[:, C1 + 1:S + 1], T.av[:, C1:S], T.cst[:, C1:S], T.fx[:, C1:C1 + 1],
+                         A.add, A.max).then_inc(sem.f1b, 1)
+    v.tensor_tensor_scan(T.bw[:, S + 14:14:-1], T.av[:, ::-1], T.cst[:], -15.0, A.add, A.max).then_inc(sem.b1, 1)
+    v.wait_ge(sem.ldsa, 16)
+    v.tensor_copy(T.sau[:], T.sai[:]).then_inc(sem.lsa, 1)
+    v.wait_ge(sem.b1, 1)
+    v.tensor_scalar(T.bc[:, 0:P1], T.bw[:, 16:P1 + 16], -1.0, 0.0, A.mult, A.max).then_inc(sem.bc0, 1)
+    for nm, k in (("lsa", 1), ("zxs", 2), ("zxd", 16), ("fa", 1), ("fb", 1), ("bc0", 1)):
+        v.wait_ge(sem[nm], k)
+    for k, (lo, hi, waits) in enumerate(((0, P1, ()), (P1, P2, ("x0", "fd", "bc1")), (P2, S, ("x1", "bc2")))):
+        for nm in waits:
+            v.wait_ge(sem[nm], 1)
+        v.tensor_tensor(T.xs[:, 0:W].indirect(T.sau[:, lo // 16:hi // 16]), T.fc[:, lo:hi], T.bc[:, lo:hi],
+                        A.add).then_inc(sem["x%d" % k], 1)
+
+    s.wait_ge(sem.z1, 1)
+    for k in range(2):
+        s.activation(T.xs[:, k * CAP:(k + 1) * CAP], T.cst[:, 0:CAP], AF.Silu).then_inc(sem.zxs, 1)
+    s.wait_ge(sem.zx0, 1)
+    s.wait_ge(sem.f1a, 1)
+    s.activation(T.fc[:, 0:C1 + 1], T.fx[:, 0:C1 + 1], AF.Relu, scale=-1.0).then_inc(sem.fa, 1)
+    s.wait_ge(sem.f1b, 1)
+    s.activation(T.fc[:, C1 + 1:2048], T.fw[:, C1 + 1:2048], AF.Relu, scale=-1.0).then_inc(sem.fb, 1)
+    s.activation(T.fc[:, 2048:S], T.fw[:, 2048:S], AF.Relu, scale=-1.0).then_inc(sem.fd, 1)
+    s.wait_ge(sem.zb, 1)
+    s.wait_ge(sem.b1, 1)
+    s.activation(T.bc[:, P1:P2], T.bw[:, P1 + 16:P2 + 16], AF.Relu, scale=-1.0).then_inc(sem.bc1, 1)
+    s.activation(T.bc[:, P2:S], T.bw[:, P2 + 16:S + 16], AF.Relu, scale=-1.0).then_inc(sem.bc2, 1)
+    s.wait_ge(sem.ifl, 32)
+    s.wait_ge(sem.iot, 1)
+    s.wait_ge(sem.lsbp, 1)
+    s.activation(T.inv[:, 0:W].indirect(T.sbp[:, 0:KS]), T.plc[:], AF.Silu).then_inc(sem.inv, 1)
+
+    g.wait_ge(sem.x2, 1)
+    used, tr = [], []
+    for r in others:
+        eng = topo.engines(core, T.cores[r])
+        far = topo.die(T.cores[r]) != topo.die(core)
+        pick = [e for e in (eng[0::2] if far else eng[1::2]) if e not in used][:4]
+        used += pick
+        tr.append(RemoteDMATransfer(dst_ids=[dst(r)], dma_engine_mask=sum(1 << e for e in pick), remote_sem=sem.arr1,
+                                    srcs=[T.xs[:, blk(r)]], dsts=[T.ys[:, blk(q)]], alu_op=0))
+    g.remote_dma_fused(tr, local_sem=sem.loc1)
+    v.wait_ge(sem.x2, 1)
+    v.tensor_copy(T.ys[:, blk(q)], T.xs[:, blk(q)]).then_inc(sem.own1, 1)
+    v.wait_ge(sem.ldb, 16)
+    v.tensor_scalar(T.bq[:], T.bv[:, 0:VS], 15.0, None, A.add).then_inc(sem.bq, 1)
+
+    te.wait_ge(sem.idt, 2)
+    te.wait_ge(sem.lda1, 16)
+    te.wait_ge(sem.lda2, 16)
+    for k in range(NQ):
+        te.matmul(T["ps%d" % (4 + k)][:, 0:CQ], T.idp[:], T.av[:, VQ + k * CQ:VQ + (k + 1) * CQ], True, False)
+    te.wait_ge(sem.ldb, 16)
+    for k in range(NS):
+        te.matmul(T["ps%d" % k][:, 0:CS], T.idm[:], T.bv[:, VS + k * CS:VS + (k + 1) * CS], True, False)
+    for k in range(NS):
+        te.wait_ge(sem["gs%d" % k], 1)
+        te.matmul(T["ps%d" % k][:, 0:CS], T.idp[:], T.gs[:, k * CS:(k + 1) * CS], False, True).then_inc(sem["pl%d" % k], 1)
+
+    for e in (v, s):
+        e.wait_ge(sem.lsb, 1)
+        e.wait_ge(sem.own1, 1)
+    v.wait_ge(sem.bq, 1)
+    for e in (v, s):
+        e.wait_ge(sem.arr1, 12)
+    v.tensor_tensor(T.ln[:, 0:VS], T.ys[:, 0:W].indirect(T.sbu[:, 0:VS // 16]), T.bq[:], A.subtract).then_inc(sem.ln, 1)
+    for k in range(NS):
+        lo = VS + k * CS
+        s.activation(T.gs[:, k * CS:(k + 1) * CS], T.ys[:, 0:W].indirect(T.sbu[:, lo // 16:(lo + CS) // 16]),
+                     AF.Identity).then_inc(sem["gs%d" % k], 1)
+    for k in range(NS):
+        lo = VS + k * CS
+        s.wait_ge(sem["pl%d" % k], 1)
+        s.activation(T.ln[:, lo:lo + CS], T["ps%d" % k][:, 0:CS], AF.Identity, bias=-15.0).then_inc(sem["lc%d" % k], 1)
+    v.wait_ge(sem.tab, 16)
+    v.tensor_scalar(T.invu[:], T.tab[:], 0.25 - OFS, None, A.add).then_inc(sem.invu, 1)
+    v.wait_ge(sem.ln, 1)
+    for k in range(NS):
+        v.wait_ge(sem["lc%d" % k], 1)
+    v.tensor_tensor_scan(T.fw[:, 1:S + 1], T.ln[:], T.cst[:], -15.0, A.add, A.min).then_inc(sem.f2, 1)
+    v.tensor_tensor_scan(T.bw[:, S + 14:14:-1], T.ln[:, ::-1], T.cst[:], -15.0, A.add, A.min).then_inc(sem.b2, 1)
+
+    fwin, bwin = T.fw[:, 0:S], T.bw[:, 16:S + 16]
+    neng = len(topo.engines(core, T.cores[others[0]]))
+    s.wait_ge(sem.invu, 1)
+    s.wait_ge(sem.zf, 1)
+    s.wait_ge(sem.f2, 1)
+    v.wait_ge(sem.invu, 1)
+    v.wait_ge(sem.zb, 1)
+    v.wait_ge(sem.b2, 1)
+    for k, r in enumerate(order):
+        cut = VB if k == 0 or r == q else CAP
+        s.activation(T.gf[:, blk(r)], fwin.indirect(lst(r)), AF.Relu, bias=30.0).then_inc(sem["gf%d" % k], 1)
+        v.tensor_scalar(T.gb[:, blk(r, 0, cut)], bwin.indirect(lst(r, 0, cut)), -30.0, 30.0,
+                        A.max, A.add).then_inc(sem["gb%d" % k], 1)
+        if k == 0:
+            s.wait_ge(sem.b2, 1)
+        if cut < CAP:
+            s.activation(T.gb[:, blk(r, cut)], bwin.indirect(lst(r, cut)), AF.Relu, bias=30.0).then_inc(sem["gc%d" % k], 1)
+        if r != q:
+            g.wait_ge(sem["gf%d" % k], 1)
+            if cut < CAP:
+                g.wait_ge(sem["gc%d" % k], 1)
+            g.wait_ge(sem["gb%d" % k], 1)
+            g.remote_dma_fused([RemoteDMATransfer(
+                dst_ids=[dst(r)], dma_engine_mask=topo.mask(core, T.cores[r]), remote_sem=sem.arr2,
+                srcs=[T.gf[:, blk(r)], T.gb[:, blk(r)]], dsts=[T.y2[:, blk(q)]], alu_op=1)], local_sem=sem.loc2)
+    v.wait_ge(sem.gf3, 1)
+    v.wait_ge(sem.gb3, 1)
+    v.tensor_tensor(T.y2[:, blk(q, 0, VB)], T.gf[:, blk(q, 0, VB)], T.gb[:, blk(q, 0, VB)], A.add).then_inc(sem.own2, 1)
+    te.wait_ge(sem.gf3, 1)
+    te.wait_ge(sem.gc3, 1)
+    te.matmul(T.ps3[:, 0:CAP - VB], T.idp[:], T.gf[:, blk(q, VB)], True, False)
+    te.matmul(T.ps3[:, 0:CAP - VB], T.idp[:], T.gb[:, blk(q, VB)], False, True).then_inc(sem.pown, 1)
+    s.wait_ge(sem.pown, 1)
+    s.activation(T.y2[:, blk(q, VB)], T.ps3[:, 0:CAP - VB], AF.Identity).then_inc(sem.own3, 1)
+
+    s.wait_ge(sem.lsa, 1)
+    for e in (v, s):
+        e.wait_ge(sem.own2, 1)
+        e.wait_ge(sem.own3, 1)
+        e.wait_ge(sem.arr2, 3 * neng)
+    ywin = T.y2[:, 0:W]
+
+    def vgather(k):
+        lo, hi = VCUT[k], VCUT[k + 1]
+        v.tensor_tensor(T.vt[:, lo:hi], ywin.indirect(T.sau[:, lo // 16:hi // 16]), T.av[:, lo:hi],
+                        A.subtract).then_inc(sem["vt%d" % k], 1)
+
+    def vturn(k):
+        lo, hi = VCUT[k], VCUT[k + 1]
+        v.wait_ge(sem["vt%d" % k], 1)
+        v.tensor_scalar(T.qv[:, lo:hi], T.vt[:, lo:hi], -1.0, 15.0, A.mult, A.add).then_inc(sem["qv%d" % k], 1)
+
+    def sgather(k):
+        lo = VQ + k * CQ
+        s.activation(T.ge[:, k * CQ:(k + 1) * CQ], ywin.indirect(T.sau[:, lo // 16:(lo + CQ) // 16]), AF.Identity,
+                     bias=15.0, scale=-1.0).then_inc(sem["ge%d" % k], 1)
+        te.wait_ge(sem["ge%d" % k], 1)
+        te.matmul(T["ps%d" % (4 + k)][:, 0:CQ], T.idp[:], T.ge[:, k * CQ:(k + 1) * CQ], False,
+                  True).then_inc(sem["pq%d" % k], 1)
+
+    def scopy(k):
+        lo = VQ + k * CQ
+        s.wait_ge(sem["pq%d" % k], 1)
+        s.activation(T.qv[:, lo:lo + CQ], T["ps%d" % (4 + k)][:, 0:CQ], AF.Identity).then_inc(sem["qs%d" % k], 1)
+
+    for step, k in ((vgather, 0), (vgather, 1), (vturn, 0), (vgather, 2), (vturn, 1), (vturn, 2),
+                    (sgather, 0), (sgather, 1), (sgather, 2), (scopy, 0), (scopy, 1), (sgather, 3), (scopy, 2), (scopy, 3)):
+        step(k)
+
+    stores = ((("qv0",), VCUT[0], VCUT[1]), (("qs0", "qs1"), VQ, VQ + 2 * CQ), (("qv1",), VCUT[1], VCUT[2]),
+              (("qv2",), VCUT[2], VCUT[3]), (("qs2", "qs3"), VQ + 2 * CQ, S))
+    for names, lo, hi in stores:
+        for nm in names:
+            sy.wait_ge(sem[nm], 1)
+        sy.dma_start(T.y[:, lo:hi], T.qv[:, lo:hi]).then_inc(sem.acc, 16)
+    g.wait_ge(sem.loc1, 12)
+    g.wait_ge(sem.loc2, 3 * neng)
+    sy.wait_ge(sem.acc, 16 * len(stores))

@@ -6,46 +6,52 @@ W = N * CAP
 K = W // 16
 KB = CAP // 16
 KS = S // 16
+HS = S // 2
 OFS = 64
-C1 = 1024
-XF = W // 2
-P1, P2 = 1152, 2624
-NS, CS = 3, 448
-VS = S - NS * CS
-NQ, CQ = 4, 448
-VQ = S - NQ * CQ
-VCUT = (0, 768, 1536, VQ)
-VB = 608
+RND = 129.0
+PR = dict(
+    ACUT=(0, 704, 1920, 4096), SA=9, SQ=(),
+    XCUT=(0, 256, 896, 2048, 4096),
+    CV=2560,
+    NS=3, CS=480,
+    AHEAD=1440,
+    UNITS=((0, 0, 384, 384, "fold"), (0, 384, 1120, 544, "fold"), (1, 0, 1120, 1120, "fold"),
+           (2, 0, 704, 704, "fold"), (2, 704, 1120, 1120, "fold"),
+           (3, 0, 512, 512, "s"), (3, 512, 832, 832, "s"), (3, 832, 1120, 1120, "s")),
+    END=((640, 0), (832, 0), (0, 512), (640, 0), (384, 448)),
+    AV=0, LAG=1,
+    C1="h", FA=832, LASTQ=0, VCAP=1, LATE=0, TS=0, CAST=1, PL=1024,
+)
 BF, F32, I32, U16 = "bfloat16", "float32", "int32", "uint16"
 
 SCRATCH = {
-    "av": ("sbuf", [128, S], BF), "bv": ("sbuf", [128, S], BF), "bq": ("sbuf", [128, VS], BF),
+    "av": ("sbuf", [128, S], BF), "bv": ("sbuf", [128, S], BF), "bq": ("sbuf", [128, S], BF),
     "cst": ("sbuf", [128, S], BF),
-    "fx": ("sbuf", [128, C1 + 16], F32),
+    "fx": ("sbuf", [128, S + 16], F32),
     "fw": ("sbuf", [128, S + 16], BF),
     "bw": ("sbuf", [128, S + 16], BF),
     "fc": ("sbuf", [128, S], BF), "bc": ("sbuf", [128, S], BF),
     "xs": ("sbuf", [128, W], BF), "ys": ("sbuf", [128, W], BF),
-    "gs": ("sbuf", [128, NS * CS], BF), "ln": ("sbuf", [128, S], BF),
+    "gs": ("sbuf", [128, 2048], BF), "ln": ("sbuf", [128, S], BF),
     "gf": ("sbuf", [128, W], BF), "gb": ("sbuf", [128, W], BF), "y2": ("sbuf", [128, W], BF),
-    "vt": ("sbuf", [128, VQ], BF), "ge": ("sbuf", [128, NQ * CQ], BF), "qv": ("sbuf", [128, S], BF),
+    "ze": ("sbuf", [128, W], BF),
+    "vt": ("sbuf", [128, S], BF), "qv": ("sbuf", [128, S], BF),
     "sai": ("sbuf", [128, KS], I32), "sbi": ("sbuf", [128, KS], I32),
-    "t1": ("sbuf", [128, KS], I32), "t3": ("sbuf", [128, KS], I32), "t4": ("sbuf", [128, KS], I32),
-    "sau": ("sbuf", [128, KS], U16), "sbu": ("sbuf", [128, KS], U16), "sbp": ("sbuf", [128, KS], U16),
-    "plc": ("sbuf", [128, S], F32), "inv": ("sbuf", [128, W], F32),
+    "saf": ("sbuf", [128, KS], F32), "uq": ("sbuf", [128, 2 * KS], BF),
+    "wu": ("sbuf", [128, 128], BF), "wq": ("sbuf", [128, 128], BF), "wo": ("sbuf", [128, 128], F32),
+    "sau": ("sbuf", [128, KS], U16), "sbu": ("sbuf", [128, KS], U16), "sam": ("sbuf", [128, KS], U16),
+    "plc": ("sbuf", [128, S], F32), "inv": ("sbuf", [128, W], F32), "zt": ("sbuf", [128, K], F32),
     "tab": ("sbuf", [128, K], F32), "invu": ("sbuf", [128, K], U16),
-    "onp": ("sbuf", [128, 128], BF), "onm": ("sbuf", [128, 128], BF),
-    "idp": ("sbuf", [128, 128], BF), "idm": ("sbuf", [128, 128], BF),
+    "onp": ("sbuf", [128, 128], BF), "idp": ("sbuf", [128, 128], BF), "idm": ("sbuf", [128, 128], BF),
 }
 for _k in range(8):
     SCRATCH["ps%d" % _k] = ("psum", [128, 512], F32)
-SEMAPHORES = ["lda1", "lda2", "ldsa", "ldsb", "ldb", "z1", "z2", "zx0", "zf", "zb", "zxs", "zxd", "l1", "l3", "l4",
-              "lsb", "lsbp", "lsa", "iot", "ifl", "ones", "idt", "f1a", "f1b", "b1", "fa", "fb", "fd", "bc0", "bc1", "bc2",
-              "x0", "x1", "x2", "own1", "arr1", "loc1", "bq", "inv", "tab", "invu", "ln", "f2", "b2",
-              "gf0", "gf1", "gf2", "gf3", "gb0", "gb1", "gb2", "gb3", "gc0", "gc3", "pown", "own2", "own3", "arr2",
-              "loc2", "acc"]
-SEMAPHORES += ["%s%d" % (n, k) for n in ("gs", "pl", "lc", "ge", "pq", "qs") for k in range(4)]
-SEMAPHORES += ["%s%d" % (n, k) for n in ("vt", "qv") for k in range(3)]
+SEMAPHORES = ["lda", "ldsa", "ldsb", "ldb", "z0", "z1", "z2", "z3", "zx0", "zf", "zb", "zxs", "zt", "wts", "parts", "pm", "gadd", "pre",
+              "lsb", "lsa", "sam", "iot0", "iot1", "ifl", "ones", "idp", "idm", "b1", "own1", "arr1", "loc1", "bq",
+              "inv0", "inv", "tab", "invu", "ln", "f2", "b2", "loc2", "acc"]
+SEMAPHORES += ["%s%d" % (n, k) for n in ("la", "fa", "fc", "bc", "x", "gs", "pl", "lc", "ge", "pq", "qs") for k in range(4)]
+SEMAPHORES += ["%s%d" % (n, k) for n in ("qv", "ar", "tn") for k in range(6)]
+SEMAPHORES += ["%s%d" % (n, k) for n in ("sg", "vg", "po", "ze") for k in range(9)]
 
 
 def rank_program(g, core, T, topo):
@@ -54,9 +60,27 @@ def rank_program(g, core, T, topo):
         return
     v, s, sy, te, sem = g.vector, g.scalar, g.sync, g.tensor, T.sem
     A = AluOpType
-    others = [r for r in range(N) if r != q]
-    others.sort(key=lambda r: (topo.die(T.cores[r]) == topo.die(core), (r - q) % N))
+    ACUT, XCUT, CV, NS, CS = (PR[k] for k in ("ACUT", "XCUT", "CV", "NS", "CS"))
+    NA, NX = len(ACUT) - 1, len(XCUT) - 1
+    VS = S - NS * CS
+    vpcs, spcs, stores, at = [], [], [], 0
+    for nv, ns in PR["END"]:
+        names = []
+        for n, pcs, nm in ((nv, vpcs, "qv%d"), (ns, spcs, "qs%d")):
+            if n:
+                names.append(nm % len(pcs))
+                pcs.append((at, at + n))
+                at += n
+        stores.append((names, at - nv - ns, at))
+    ADD = S - at
+
+    def far_first(r):
+        rest = [x for x in range(N) if x != r]
+        return sorted(rest, key=lambda x: (topo.die(T.cores[x]) == topo.die(T.cores[r]), x ^ r))
+
+    others = far_first(q)
     order = others + [q]
+    eng = topo.engines(core, T.cores[others[0]])
 
     def blk(r, lo=0, hi=CAP):
         return slice(r * CAP + lo, r * CAP + hi)
@@ -68,202 +92,267 @@ def rank_program(g, core, T, topo):
         rid, pid, _ = topo.addr(T.cores[r])
         return DstId(rid=rid, pnc=pid)
 
-    sy.dma_start(T.av[:, 0:C1], T.a[:, 0:C1]).then_inc(sem.lda1, 16)
-    sy.dma_start(T.sbi[:], T.sb[:]).then_inc(sem.ldsb, 16)
-    sy.dma_start(T.av[:, C1:S], T.a[:, C1:S]).then_inc(sem.lda2, 16)
+    def wait(e, *names):
+        for nm in names:
+            nm, k = nm if isinstance(nm, tuple) else (nm, 1)
+            e.wait_ge(sem[nm], k)
+
+    def ps(k):
+        return T["ps%d" % k]
+
+    for k in range(NA):
+        sy.dma_start(T.xs[:, ACUT[k]:ACUT[k + 1]], T.a[:, ACUT[k]:ACUT[k + 1]]).then_inc(sem["la%d" % k], 16)
+    lsa, lsb, sai = "lsa", "lsb", T.sau
     sy.dma_start(T.sai[:], T.sa[:]).then_inc(sem.ldsa, 16)
-    sy.dma_start(T.xs[:, XF:W], T.b[:, 0:W - XF]).then_inc(sem.zxd, 16)
+    sy.dma_start(T.sbi[:], T.sb[:]).then_inc(sem.ldsb, 16)
+    wait(sy, "zt")
+    sy.dma_start(T.inv[0:128:16, :], T.zt[:]).then_inc(sem.ifl, 16)
     sy.dma_start(T.bv[:], T.b[:]).then_inc(sem.ldb, 16)
-    sy.wait_ge(sem.inv, 1)
-    sy.dma_start(T.tab[:], T.inv[0:128:16, :]).then_inc(sem.tab, 16)
+    sy.dma_start(T.av[:], T.a[:]).then_inc(sem.lda, 16)
+    wait(sy, "inv")
+    for r in order:
+        sy.dma_start(T.tab[:, r * KB:(r + 1) * KB], T.inv[0:128:16, blk(r)]).then_inc(sem.tab, 16)
 
-    g.dma_start(T.inv[0:128:16, 0:S], T.a[0:8, :]).then_inc(sem.ifl, 16)
-    g.dma_start(T.inv[0:128:16, S:W], T.a[0:8, 0:W - S]).then_inc(sem.ifl, 16)
-    g.iota(T.plc[:], [[1, S]], OFS, 0, allow_small_or_imprecise_dtypes=True).then_inc(sem.iot, 1)
-    g.iota(T.onp[:], [[0, 128]], 1, 0, allow_small_or_imprecise_dtypes=True).then_inc(sem.ones, 1)
-    g.iota(T.onm[:], [[0, 128]], -1, 0, allow_small_or_imprecise_dtypes=True).then_inc(sem.ones, 1)
-    g.wait_ge(sem.ones, 2)
-    g.affine_select(T.idp[:], T.onp[:], [[-1, 128]], A.is_equal, 0.0, 0, 1).then_inc(sem.idt, 1)
-    g.affine_select(T.idm[:], T.onm[:], [[-1, 128]], A.is_equal, 0.0, 0, 1).then_inc(sem.idt, 1)
+    g.iota(T.cst[:, CV:S], [[0, S - CV]], -15, 0, allow_small_or_imprecise_dtypes=True).then_inc(sem.z2, 1)
+    g.iota(T.xs[:, S:W], [[0, W - S]], 0, 0, allow_small_or_imprecise_dtypes=True).then_inc(sem.zxs, 1)
+    for k in range(2):
+        g.iota(T.plc[:, k * HS:(k + 1) * HS], [[1, HS]], OFS + k * HS, 0,
+               allow_small_or_imprecise_dtypes=True).then_inc(sem["iot%d" % k], 1)
+    wait(g, "ones")
+    g.affine_select(T.idp[:], T.onp[:], [[-1, 128]], A.is_equal, 0.0, 0, 1).then_inc(sem.idp, 1)
 
-    v.memset(T.cst[:, 0:CAP], -15.0).then_inc(sem.z1, 1)
+    v.memset(T.cst[:, 0:K], -15.0).then_inc(sem.z0, 1)
+    v.memset(T.cst[:, K:CV], -15.0).then_inc(sem.z1, 1)
     v.memset(T.fx[:, 0:1], -15.0).then_inc(sem.zx0, 1)
-    v.memset(T.cst[:, CAP:S], -15.0).then_inc(sem.z2, 1)
-    v.memset(T.fw[:, 0:1], -15.0).then_inc(sem.zf, 1)
     v.memset(T.bw[:, S + 15:S + 16], -15.0).then_inc(sem.zb, 1)
-    v.wait_ge(sem.z1, 1)
-    v.wait_ge(sem.lda1, 16)
-    v.tensor_tensor_scan(T.fx[:, 1:C1 + 1], T.av[:, 0:C1], T.cst[:, 0:C1], -15.0, A.add, A.max).then_inc(sem.f1a, 1)
-    v.wait_ge(sem.ldsb, 16)
-    v.tensor_scalar(T.t1[:], T.sbi[:], 15, None, A.bitwise_and).then_inc(sem.l1, 1)
-    v.tensor_copy(T.sbu[:], T.sbi[:]).then_inc(sem.lsb, 1)
-    v.wait_ge(sem.l1, 1)
-    v.tensor_scalar(T.t3[:], T.t1[:], 16 * K - 1, None, A.mult).then_inc(sem.l3, 1)
-    v.wait_ge(sem.l3, 1)
-    v.tensor_tensor(T.t4[:], T.t3[:], T.sbi[:], A.add).then_inc(sem.l4, 1)
-    v.wait_ge(sem.l4, 1)
-    v.tensor_scalar(T.sbp[:], T.t4[:], 0.0625, None, A.mult).then_inc(sem.lsbp, 1)
-    v.wait_ge(sem.z2, 1)
-    v.wait_ge(sem.f1a, 1)
-    v.wait_ge(sem.lda2, 16)
-    v.tensor_tensor_scan(T.fw[:, C1 + 1:S + 1], T.av[:, C1:S], T.cst[:, C1:S], T.fx[:, C1:C1 + 1],
-                         A.add, A.max).then_inc(sem.f1b, 1)
-    v.tensor_tensor_scan(T.bw[:, S + 14:14:-1], T.av[:, ::-1], T.cst[:], -15.0, A.add, A.max).then_inc(sem.b1, 1)
-    v.wait_ge(sem.ldsa, 16)
+    v.memset(T.onp[:], 1.0).then_inc(sem.ones, 1)
+    wait(v, "z0", "z1")
+    for k in range(NA):
+        lo, hi = ACUT[k], ACUT[k + 1]
+        wait(v, ("la%d" % k, 16))
+        if k:
+            wait(v, "fa%d" % (k - 1))
+        out = T.fx if k < NA - 1 else T.fw
+        v.tensor_tensor_scan(out[:, lo + 1:hi + 1], T.xs[:, lo:hi], T.cst[:, 0:hi - lo], T.fx[:, lo:lo + 1] if k else -15.0,
+                             A.add, A.max).then_inc(sem["fa%d" % k], 1)
+    wait(v, "z2")
+    v.tensor_tensor_scan(T.bw[:, S + 14:14:-1], T.xs[:, S - 1::-1], T.cst[:], -15.0, A.add, A.max).then_inc(sem.b1, 1)
+    wait(v, ("ldsa", 16))
     v.tensor_copy(T.sau[:], T.sai[:]).then_inc(sem.lsa, 1)
-    v.wait_ge(sem.b1, 1)
-    v.tensor_scalar(T.bc[:, 0:P1], T.bw[:, 16:P1 + 16], -1.0, 0.0, A.mult, A.max).then_inc(sem.bc0, 1)
-    for nm, k in (("lsa", 1), ("zxs", 2), ("zxd", 16), ("fa", 1), ("fb", 1), ("bc0", 1)):
-        v.wait_ge(sem[nm], k)
-    for k, (lo, hi, waits) in enumerate(((0, P1, ()), (P1, P2, ("x0", "fd", "bc1")), (P2, S, ("x1", "bc2")))):
-        for nm in waits:
-            v.wait_ge(sem[nm], 1)
+    wait(v, ("ldsb", 16))
+    v.tensor_copy(T.sbu[:], T.sbi[:]).then_inc(sem.lsb, 1)
+    wait(v, "b1", lsa, "zxs")
+    for k in range(NX):
+        lo, hi = XCUT[k], XCUT[k + 1]
+        wait(v, "bc%d" % k, *["fc%d" % j for j in range(NA) if ACUT[j] < hi])
+        if k:
+            wait(v, "x%d" % (k - 1))
+        else:
+            wait(v, "fa%d" % (NA - 1))
         v.tensor_tensor(T.xs[:, 0:W].indirect(T.sau[:, lo // 16:hi // 16]), T.fc[:, lo:hi], T.bc[:, lo:hi],
                         A.add).then_inc(sem["x%d" % k], 1)
+    xlast = "x%d" % (NX - 1)
 
-    s.wait_ge(sem.z1, 1)
-    for k in range(2):
-        s.activation(T.xs[:, k * CAP:(k + 1) * CAP], T.cst[:, 0:CAP], AF.Silu).then_inc(sem.zxs, 1)
-    s.wait_ge(sem.zx0, 1)
-    s.wait_ge(sem.f1a, 1)
-    s.activation(T.fc[:, 0:C1 + 1], T.fx[:, 0:C1 + 1], AF.Relu, scale=-1.0).then_inc(sem.fa, 1)
-    s.wait_ge(sem.f1b, 1)
-    s.activation(T.fc[:, C1 + 1:2048], T.fw[:, C1 + 1:2048], AF.Relu, scale=-1.0).then_inc(sem.fb, 1)
-    s.activation(T.fc[:, 2048:S], T.fw[:, 2048:S], AF.Relu, scale=-1.0).then_inc(sem.fd, 1)
-    s.wait_ge(sem.zb, 1)
-    s.wait_ge(sem.b1, 1)
-    s.activation(T.bc[:, P1:P2], T.bw[:, P1 + 16:P2 + 16], AF.Relu, scale=-1.0).then_inc(sem.bc1, 1)
-    s.activation(T.bc[:, P2:S], T.bw[:, P2 + 16:S + 16], AF.Relu, scale=-1.0).then_inc(sem.bc2, 1)
-    s.wait_ge(sem.ifl, 32)
-    s.wait_ge(sem.iot, 1)
-    s.wait_ge(sem.lsbp, 1)
-    s.activation(T.inv[:, 0:W].indirect(T.sbp[:, 0:KS]), T.plc[:], AF.Silu).then_inc(sem.inv, 1)
+    wait(s, "z0")
+    s.activation(T.zt[:], T.cst[:, 0:K], AF.Silu).then_inc(sem.zt, 1)
+    wait(s, "zx0")
+    for k in range(NA):
+        lo, hi = (ACUT[k] + 1 if k else 0), min(ACUT[k + 1] + 1, S)
+        wait(s, "fa%d" % k)
+        src = T.fx if k < NA - 1 else T.fw
+        s.activation(T.fc[:, lo:hi], src[:, lo:hi], AF.Relu, scale=-1.0).then_inc(sem["fc%d" % k], 1)
+    wait(s, "zb", "b1")
+    for k in range(NX):
+        lo, hi = XCUT[k], XCUT[k + 1]
+        s.activation(T.bc[:, lo:hi], T.bw[:, lo + 16:hi + 16], AF.Relu, scale=-1.0).then_inc(sem["bc%d" % k], 1)
+    wait(s, ("ifl", 16), "iot0", lsb)
+    s.activation(T.inv[:, 0:W].indirect(T.sbu[:, 0:KS // 2]), T.plc[:, 0:HS], AF.Silu).then_inc(sem.inv0, 1)
+    wait(s, "inv0", "iot1")
+    s.activation(T.inv[:, 0:W].indirect(T.sbu[:, KS // 2:KS]), T.plc[:, HS:S], AF.Silu).then_inc(sem.inv, 1)
 
-    g.wait_ge(sem.x2, 1)
-    used, tr = [], []
-    for r in others:
-        eng = topo.engines(core, T.cores[r])
-        far = topo.die(T.cores[r]) != topo.die(core)
-        pick = [e for e in (eng[0::2] if far else eng[1::2]) if e not in used][:4]
-        used += pick
-        tr.append(RemoteDMATransfer(dst_ids=[dst(r)], dma_engine_mask=sum(1 << e for e in pick), remote_sem=sem.arr1,
-                                    srcs=[T.xs[:, blk(r)]], dsts=[T.ys[:, blk(q)]], alu_op=0))
-    g.remote_dma_fused(tr, local_sem=sem.loc1)
-    v.wait_ge(sem.x2, 1)
+    ev, od = eng[0::2], eng[1::2]
+    h = len(ev) // 2
+    FA = PR["FA"]
+    calls = {"b": [[(0, 0, CAP, ev), (1, 0, CAP, od)], [(2, 0, CAP, eng)]],
+             "d": [[(0, 0, CAP, ev[:h]), (1, 0, CAP, ev[h:])], [(2, 0, CAP, od)]],
+             "h": [[(0, 0, FA, ev[:h]), (1, 0, FA, ev[h:])], [(2, 0, CAP, od)],
+                   [(0, FA, CAP, od[:h]), (1, FA, CAP, od[h:])]]}[PR["C1"]]
+    wait(g, xlast)
+    for c in calls:
+        g.remote_dma_fused([RemoteDMATransfer(
+            dst_ids=[dst(others[k])], dma_engine_mask=sum(1 << e for e in p), remote_sem=sem.arr1,
+            srcs=[T.xs[:, blk(others[k], lo, hi)]], dsts=[T.ys[:, blk(q, lo, hi)]], alu_op=0) for k, lo, hi, p in c],
+            local_sem=sem.loc1)
+    n1 = narr = sum(len(p) for c in calls for _, _, _, p in c)
+    if ADD:
+        g.dma_start(T.y[:, S - ADD:S], T.a[:, S - ADD:S]).then_inc(sem.pre, 16)
+    wait(v, xlast)
     v.tensor_copy(T.ys[:, blk(q)], T.xs[:, blk(q)]).then_inc(sem.own1, 1)
-    v.wait_ge(sem.ldb, 16)
-    v.tensor_scalar(T.bq[:], T.bv[:, 0:VS], 15.0, None, A.add).then_inc(sem.bq, 1)
+    v.memset(T.fw[:, 0:1], -15.0).then_inc(sem.zf, 1)
+    wait(v, "idp")
+    for w, c in ((T.idm, -1.0), (T.wu, -float(CAP)), (T.wq, CAP - 16.0), (T.wo, 16.0)):
+        v.tensor_scalar(w[:], T.idp[:], c, None, A.mult).then_inc(sem.wts, 1)
+    v.tensor_copy(T.saf[:], sai[:]).then_inc(sem.parts, 1)
+    v.tensor_scalar(T.uq[:, 0:KS], sai[:], 1.0 / KB, RND + 0.5 / KB - 0.5, A.mult, A.add).then_inc(sem.parts, 1)
+    v.tensor_scalar(T.uq[:, KS:2 * KS], sai[:], 1.0 / CAP, RND + 0.5 / CAP - 0.5, A.mult, A.add).then_inc(sem.parts, 1)
+    wait(v, ("ldb", 16))
+    v.tensor_scalar(T.bq[:, 0:VS], T.bv[:, 0:VS], 15.0, None, A.add).then_inc(sem.bq, 1)
+    wait(v, "pm")
+    v.tensor_scalar(T.sam[:], ps(3)[:, 0:KS], RND * 15.0, None, A.add).then_inc(sem.sam, 1)
 
-    te.wait_ge(sem.idt, 2)
-    te.wait_ge(sem.lda1, 16)
-    te.wait_ge(sem.lda2, 16)
-    for k in range(NQ):
-        te.matmul(T["ps%d" % (4 + k)][:, 0:CQ], T.idp[:], T.av[:, VQ + k * CQ:VQ + (k + 1) * CQ], True, False)
-    te.wait_ge(sem.ldb, 16)
+    wait(te, ("wts", 4), ("ldb", 16))
     for k in range(NS):
-        te.matmul(T["ps%d" % k][:, 0:CS], T.idm[:], T.bv[:, VS + k * CS:VS + (k + 1) * CS], True, False)
+        te.matmul(ps(k)[:, 0:CS], T.idm[:], T.bv[:, VS + k * CS:VS + (k + 1) * CS], True, False)
+    wait(te, ("parts", 3))
+    te.matmul(ps(3)[:, 0:KS], T.wo[:], T.saf[:], True, False)
+    te.matmul(ps(3)[:, 0:KS], T.wu[:], T.uq[:, 0:KS], False, False)
+    te.matmul(ps(3)[:, 0:KS], T.idp[:], T.uq[:, 0:KS], False, False)
+    te.matmul(ps(3)[:, 0:KS], T.wq[:], T.uq[:, KS:2 * KS], False, True).then_inc(sem.pm, 1)
     for k in range(NS):
-        te.wait_ge(sem["gs%d" % k], 1)
-        te.matmul(T["ps%d" % k][:, 0:CS], T.idp[:], T.gs[:, k * CS:(k + 1) * CS], False, True).then_inc(sem["pl%d" % k], 1)
+        wait(te, "gs%d" % k)
+        te.matmul(ps(k)[:, 0:CS], T.idp[:], T.gs[:, k * CS:(k + 1) * CS], False, True).then_inc(sem["pl%d" % k], 1)
+    wait(te, ("lda", 16))
+    for k, (lo, hi) in enumerate(spcs):
+        te.matmul(ps(4 + k)[:, 0:hi - lo], T.idp[:], T.av[:, lo:hi], True, False)
 
+    wait(v, "bq")
     for e in (v, s):
-        e.wait_ge(sem.lsb, 1)
-        e.wait_ge(sem.own1, 1)
-    v.wait_ge(sem.bq, 1)
-    for e in (v, s):
-        e.wait_ge(sem.arr1, 12)
-    v.tensor_tensor(T.ln[:, 0:VS], T.ys[:, 0:W].indirect(T.sbu[:, 0:VS // 16]), T.bq[:], A.subtract).then_inc(sem.ln, 1)
+        wait(e, lsb, "own1", ("arr1", narr))
+    v.tensor_tensor(T.ln[:, 0:VS], T.ys[:, 0:W].indirect(T.sbu[:, 0:VS // 16]), T.bq[:, 0:VS], A.subtract).then_inc(sem.ln, 1)
     for k in range(NS):
         lo = VS + k * CS
         s.activation(T.gs[:, k * CS:(k + 1) * CS], T.ys[:, 0:W].indirect(T.sbu[:, lo // 16:(lo + CS) // 16]),
                      AF.Identity).then_inc(sem["gs%d" % k], 1)
     for k in range(NS):
         lo = VS + k * CS
-        s.wait_ge(sem["pl%d" % k], 1)
-        s.activation(T.ln[:, lo:lo + CS], T["ps%d" % k][:, 0:CS], AF.Identity, bias=-15.0).then_inc(sem["lc%d" % k], 1)
-    v.wait_ge(sem.tab, 16)
-    v.tensor_scalar(T.invu[:], T.tab[:], 0.25 - OFS, None, A.add).then_inc(sem.invu, 1)
-    v.wait_ge(sem.ln, 1)
-    for k in range(NS):
-        v.wait_ge(sem["lc%d" % k], 1)
+        wait(s, "pl%d" % k)
+        s.activation(T.ln[:, lo:lo + CS], ps(k)[:, 0:CS], AF.Identity, bias=-15.0).then_inc(sem["lc%d" % k], 1)
+    if not PR["LATE"]:
+        wait(v, ("tab", 16 * N))
+        v.tensor_scalar(T.invu[:], T.tab[:], 0.25 - OFS, None, A.add).then_inc(sem.invu, 1)
+    wait(v, "ln", *["lc%d" % k for k in range(NS)])
     v.tensor_tensor_scan(T.fw[:, 1:S + 1], T.ln[:], T.cst[:], -15.0, A.add, A.min).then_inc(sem.f2, 1)
+    if PR["LATE"]:
+        wait(v, ("tab", 16 * N))
+        v.tensor_scalar(T.invu[:], T.tab[:], 0.25 - OFS, None, A.add).then_inc(sem.invu, 1)
     v.tensor_tensor_scan(T.bw[:, S + 14:14:-1], T.ln[:, ::-1], T.cst[:], -15.0, A.add, A.min).then_inc(sem.b2, 1)
 
     fwin, bwin = T.fw[:, 0:S], T.bw[:, 16:S + 16]
-    neng = len(topo.engines(core, T.cores[others[0]]))
-    s.wait_ge(sem.invu, 1)
-    s.wait_ge(sem.zf, 1)
-    s.wait_ge(sem.f2, 1)
-    v.wait_ge(sem.invu, 1)
-    v.wait_ge(sem.zb, 1)
-    v.wait_ge(sem.b2, 1)
-    for k, r in enumerate(order):
-        cut = VB if k == 0 or r == q else CAP
-        s.activation(T.gf[:, blk(r)], fwin.indirect(lst(r)), AF.Relu, bias=30.0).then_inc(sem["gf%d" % k], 1)
-        v.tensor_scalar(T.gb[:, blk(r, 0, cut)], bwin.indirect(lst(r, 0, cut)), -30.0, 30.0,
-                        A.max, A.add).then_inc(sem["gb%d" % k], 1)
-        if k == 0:
-            s.wait_ge(sem.b2, 1)
-        if cut < CAP:
-            s.activation(T.gb[:, blk(r, cut)], bwin.indirect(lst(r, cut)), AF.Relu, bias=30.0).then_inc(sem["gc%d" % k], 1)
-        if r != q:
-            g.wait_ge(sem["gf%d" % k], 1)
-            if cut < CAP:
-                g.wait_ge(sem["gc%d" % k], 1)
-            g.wait_ge(sem["gb%d" % k], 1)
-            g.remote_dma_fused([RemoteDMATransfer(
-                dst_ids=[dst(r)], dma_engine_mask=topo.mask(core, T.cores[r]), remote_sem=sem.arr2,
-                srcs=[T.gf[:, blk(r)], T.gb[:, blk(r)]], dsts=[T.y2[:, blk(q)]], alu_op=1)], local_sem=sem.loc2)
-    v.wait_ge(sem.gf3, 1)
-    v.wait_ge(sem.gb3, 1)
-    v.tensor_tensor(T.y2[:, blk(q, 0, VB)], T.gf[:, blk(q, 0, VB)], T.gb[:, blk(q, 0, VB)], A.add).then_inc(sem.own2, 1)
-    te.wait_ge(sem.gf3, 1)
-    te.wait_ge(sem.gc3, 1)
-    te.matmul(T.ps3[:, 0:CAP - VB], T.idp[:], T.gf[:, blk(q, VB)], True, False)
-    te.matmul(T.ps3[:, 0:CAP - VB], T.idp[:], T.gb[:, blk(q, VB)], False, True).then_inc(sem.pown, 1)
-    s.wait_ge(sem.pown, 1)
-    s.activation(T.y2[:, blk(q, VB)], T.ps3[:, 0:CAP - VB], AF.Identity).then_inc(sem.own3, 1)
+    wait(s, "invu", "zf", "zb", "f2")
+    wait(v, "invu", "zb", "b2")
+    wait(te, "sam", *["lc%d" % k for k in range(NS)])
+    units = PR["UNITS"]
+    banks = [0, 1, 2, 3, 6, 7]
+    ahead, at, cnt = [], 0, [0] * len(units)
+    for b, lo, hi, vb, how in units:
+        ahead.append(min(hi, lo + max(0, PR["AHEAD"] - at)))
+        at += hi - lo
 
-    s.wait_ge(sem.lsa, 1)
+    def sget(kind, k, lo, hi):
+        if lo < hi:
+            r = order[units[k][0]]
+            out, win = (T.gf, fwin) if kind == "F" else (T.gb, bwin)
+            s.activation(out[:, blk(r, lo, hi)], win.indirect(lst(r, lo, hi)), AF.Relu, bias=30.0).then_inc(sem["sg%d" % k], 1)
+            cnt[k] += 1
+
+    def send(k):
+        b, lo, hi, vb, how = units[k]
+        r = order[b]
+        srcs = [T.gf, T.gb] if how == "fold" else [T.ze]
+        g.remote_dma_fused([RemoteDMATransfer(
+            dst_ids=[dst(r)], dma_engine_mask=topo.mask(core, T.cores[r]), remote_sem=sem["ar%d" % k],
+            srcs=[t[:, blk(r, lo, hi)] for t in srcs], dsts=[T.y2[:, blk(q, lo, hi)]], alu_op=len(srcs) - 1)],
+            local_sem=sem.loc2)
+
+    def copy_out(k):
+        b, lo, hi, vb, how = units[k]
+        out = (T.y2 if b == 3 else T.ze)[:, blk(order[b], lo, hi)]
+        src = ps(bank[k])[:, 0:hi - lo]
+        if how == "s":
+            wait(s, "po%d" % k)
+            s.activation(out, src, AF.Identity, bias=15.0).then_inc(sem["ze%d" % k], 1)
+        else:
+            wait(v, "po%d" % k)
+            v.tensor_scalar(out, src, 15.0, None, A.add).then_inc(sem["ze%d" % k], 1)
+        if b < 3:
+            wait(g, "ze%d" % k)
+            send(k)
+
+    for k, u in enumerate(units):
+        sget("F", k, u[1], ahead[k])
+    wait(s, "b2")
+    bank, due = {}, []
+    for k, (b, lo, hi, vb, how) in enumerate(units):
+        r = order[b]
+        sget("F", k, ahead[k], hi)
+        sget("B", k, vb, hi)
+        v.tensor_scalar(T.gb[:, blk(r, lo, vb)], bwin.indirect(lst(r, lo, vb)), -30.0, 30.0,
+                        A.max, A.add).then_inc(sem["vg%d" % k], 1)
+        for j in due:
+            copy_out(j)
+        due = []
+        if how == "fold":
+            wait(g, ("sg%d" % k, cnt[k]), "vg%d" % k)
+            send(k)
+        else:
+            bank[k] = banks.pop(0)
+            wait(te, ("sg%d" % k, cnt[k]), "vg%d" % k)
+            te.matmul(ps(bank[k])[:, 0:hi - lo], T.idm[:], T.gf[:, blk(r, lo, hi)], True, False)
+            te.matmul(ps(bank[k])[:, 0:hi - lo], T.idm[:], T.gb[:, blk(r, lo, hi)], False, True).then_inc(sem["po%d" % k], 1)
+            due.append(k)
+    for j in due:
+        copy_out(j)
+    n2 = len(eng) * sum(u[0] < 3 for u in units)
+    ready = []
+    for k, (b, lo, hi, vb, how) in enumerate(units):
+        if b == 3:
+            ready.append("ze%d" % k)
+        elif how == "fold":
+            part = T.y2[:, blk([x for x in others if far_first(x)[b] == q][0], lo, hi)]
+            wait(v, ("ar%d" % k, len(eng)))
+            v.tensor_scalar(part, part, -1.0, 15.0, A.mult, A.add).then_inc(sem["tn%d" % k], 1)
+            ready.append("tn%d" % k)
+        else:
+            ready.append(("ar%d" % k, len(eng)))
+
+    wait(v, ("lda", 16))
     for e in (v, s):
-        e.wait_ge(sem.own2, 1)
-        e.wait_ge(sem.own3, 1)
-        e.wait_ge(sem.arr2, 3 * neng)
+        wait(e, "sam", *ready)
     ywin = T.y2[:, 0:W]
 
     def vgather(k):
-        lo, hi = VCUT[k], VCUT[k + 1]
-        v.tensor_tensor(T.vt[:, lo:hi], ywin.indirect(T.sau[:, lo // 16:hi // 16]), T.av[:, lo:hi],
-                        A.subtract).then_inc(sem["vt%d" % k], 1)
-
-    def vturn(k):
-        lo, hi = VCUT[k], VCUT[k + 1]
-        v.wait_ge(sem["vt%d" % k], 1)
-        v.tensor_scalar(T.qv[:, lo:hi], T.vt[:, lo:hi], -1.0, 15.0, A.mult, A.add).then_inc(sem["qv%d" % k], 1)
+        lo, hi = vpcs[k]
+        v.tensor_tensor(T.qv[:, lo:hi], ywin.indirect(T.sam[:, lo // 16:hi // 16]), T.av[:, lo:hi],
+                        A.add).then_inc(sem["qv%d" % k], 1)
 
     def sgather(k):
-        lo = VQ + k * CQ
-        s.activation(T.ge[:, k * CQ:(k + 1) * CQ], ywin.indirect(T.sau[:, lo // 16:(lo + CQ) // 16]), AF.Identity,
-                     bias=15.0, scale=-1.0).then_inc(sem["ge%d" % k], 1)
-        te.wait_ge(sem["ge%d" % k], 1)
-        te.matmul(T["ps%d" % (4 + k)][:, 0:CQ], T.idp[:], T.ge[:, k * CQ:(k + 1) * CQ], False,
-                  True).then_inc(sem["pq%d" % k], 1)
+        lo, hi = spcs[k]
+        s.activation(T.vt[:, lo:hi], ywin.indirect(T.sam[:, lo // 16:hi // 16]), AF.Identity).then_inc(sem["ge%d" % k], 1)
+        wait(te, "ge%d" % k)
+        te.matmul(ps(4 + k)[:, 0:hi - lo], T.idp[:], T.vt[:, lo:hi], False, True).then_inc(sem["pq%d" % k], 1)
 
     def scopy(k):
-        lo = VQ + k * CQ
-        s.wait_ge(sem["pq%d" % k], 1)
-        s.activation(T.qv[:, lo:lo + CQ], T["ps%d" % (4 + k)][:, 0:CQ], AF.Identity).then_inc(sem["qs%d" % k], 1)
+        lo, hi = spcs[k]
+        wait(s, "pq%d" % k)
+        s.activation(T.qv[:, lo:hi], ps(4 + k)[:, 0:hi - lo], AF.Identity).then_inc(sem["qs%d" % k], 1)
 
-    for step, k in ((vgather, 0), (vgather, 1), (vturn, 0), (vgather, 2), (vturn, 1), (vturn, 2),
-                    (sgather, 0), (sgather, 1), (sgather, 2), (scopy, 0), (scopy, 1), (sgather, 3), (scopy, 2), (scopy, 3)):
-        step(k)
+    if ADD:
+        s.activation(T.vt[:, S - ADD:S], ywin.indirect(T.sam[:, (S - ADD) // 16:KS]), AF.Identity).then_inc(sem.gadd, 1)
+        wait(g, "gadd", ("pre", 16))
+        g.dma_start(T.y[:, S - ADD:S], T.vt[:, S - ADD:S], accum_op=A.add).then_inc(sem.pre, 16)
+        wait(g, ("pre", 32))
+    for k in range(len(vpcs)):
+        vgather(k)
+    lag = PR["LAG"]
+    for j in range(len(spcs) + lag):
+        if j < len(spcs):
+            sgather(j)
+        if j >= lag:
+            scopy(j - lag)
 
-    stores = ((("qv0",), VCUT[0], VCUT[1]), (("qs0", "qs1"), VQ, VQ + 2 * CQ), (("qv1",), VCUT[1], VCUT[2]),
-              (("qv2",), VCUT[2], VCUT[3]), (("qs2", "qs3"), VQ + 2 * CQ, S))
-    for names, lo, hi in stores:
-        for nm in names:
-            sy.wait_ge(sem[nm], 1)
-        sy.dma_start(T.y[:, lo:hi], T.qv[:, lo:hi]).then_inc(sem.acc, 16)
-    g.wait_ge(sem.loc1, 12)
-    g.wait_ge(sem.loc2, 3 * neng)
-    sy.wait_ge(sem.acc, 16 * len(stores))
+    for j, (names, lo, hi) in enumerate(stores):
+        e = s if PR["LASTQ"] and j == len(stores) - 1 else sy
+        wait(e, *names)
+        e.dma_start(T.y[:, lo:hi], T.qv[:, lo:hi]).then_inc(sem.acc, 16)
+    wait(g, ("loc1", n1), ("loc2", n2))
+    wait(sy, ("acc", 16 * len(stores)))

from concourse.bass import DstId, RemoteDMATransfer
from concourse.mybir import AluOpType, ActivationFunctionType as AF

S, CAP, N = 4096, 1120, 4
W = N * CAP
K = W // 16
KB = CAP // 16
KS = S // 16
HS = S // 2
OFS = 64
RND = 129.0
PR = dict(
    ACUT=(0, 704, 1920, 4096), SA=9, SQ=(),
    XCUT=(0, 256, 896, 2048, 4096),
    CV=2560,
    NS=3, CS=480,
    AHEAD=1440,
    UNITS=((0, 0, 384, 384, "fold"), (0, 384, 1120, 544, "fold"), (1, 0, 1120, 1120, "fold"),
           (2, 0, 704, 704, "fold"), (2, 704, 1120, 1120, "fold"),
           (3, 0, 512, 512, "s"), (3, 512, 832, 832, "s"), (3, 832, 1120, 1120, "s")),
    END=((640, 0), (832, 0), (0, 512), (640, 0), (384, 448)),
    AV=0, LAG=1,
    C1="h", FA=832, LASTQ=0, VCAP=1, LATE=0, TS=0, CAST=1, PL=1024,
)
BF, F32, I32, U16 = "bfloat16", "float32", "int32", "uint16"

SCRATCH = {
    "av": ("sbuf", [128, S], BF), "bv": ("sbuf", [128, S], BF), "bq": ("sbuf", [128, S], BF),
    "cst": ("sbuf", [128, S], BF),
    "fx": ("sbuf", [128, S + 16], F32),
    "fw": ("sbuf", [128, S + 16], BF),
    "bw": ("sbuf", [128, S + 16], BF),
    "fc": ("sbuf", [128, S], BF), "bc": ("sbuf", [128, S], BF),
    "xs": ("sbuf", [128, W], BF), "ys": ("sbuf", [128, W], BF),
    "gs": ("sbuf", [128, 2048], BF), "ln": ("sbuf", [128, S], BF),
    "gf": ("sbuf", [128, W], BF), "gb": ("sbuf", [128, W], BF), "y2": ("sbuf", [128, W], BF),
    "ze": ("sbuf", [128, W], BF),
    "vt": ("sbuf", [128, S], BF), "qv": ("sbuf", [128, S], BF),
    "sai": ("sbuf", [128, KS], I32), "sbi": ("sbuf", [128, KS], I32),
    "saf": ("sbuf", [128, KS], F32), "uq": ("sbuf", [128, 2 * KS], BF),
    "wu": ("sbuf", [128, 128], BF), "wq": ("sbuf", [128, 128], BF), "wo": ("sbuf", [128, 128], F32),
    "sau": ("sbuf", [128, KS], U16), "sbu": ("sbuf", [128, KS], U16), "sam": ("sbuf", [128, KS], U16),
    "plc": ("sbuf", [128, S], F32), "inv": ("sbuf", [128, W], F32), "zt": ("sbuf", [128, K], F32),
    "tab": ("sbuf", [128, K], F32), "invu": ("sbuf", [128, K], U16),
    "onp": ("sbuf", [128, 128], BF), "idp": ("sbuf", [128, 128], BF), "idm": ("sbuf", [128, 128], BF),
}
for _k in range(8):
    SCRATCH["ps%d" % _k] = ("psum", [128, 512], F32)
SEMAPHORES = ["lda", "ldsa", "ldsb", "ldb", "z0", "z1", "z2", "z3", "zx0", "zf", "zb", "zxs", "zt", "wts", "parts", "pm", "gadd", "pre",
              "lsb", "lsa", "sam", "iot0", "iot1", "ifl", "ones", "idp", "idm", "b1", "own1", "arr1", "loc1", "bq",
              "inv0", "inv", "tab", "invu", "ln", "f2", "b2", "loc2", "acc"]
SEMAPHORES += ["%s%d" % (n, k) for n in ("la", "fa", "fc", "bc", "x", "gs", "pl", "lc", "ge", "pq", "qs") for k in range(4)]
SEMAPHORES += ["%s%d" % (n, k) for n in ("qv", "ar", "tn") for k in range(6)]
SEMAPHORES += ["%s%d" % (n, k) for n in ("sg", "vg", "po", "ze") for k in range(9)]


def rank_program(g, core, T, topo):
    q = T.rank_of(core)
    if q is None:
        return
    v, s, sy, te, sem = g.vector, g.scalar, g.sync, g.tensor, T.sem
    A = AluOpType
    ACUT, XCUT, CV, NS, CS = (PR[k] for k in ("ACUT", "XCUT", "CV", "NS", "CS"))
    NA, NX = len(ACUT) - 1, len(XCUT) - 1
    VS = S - NS * CS
    vpcs, spcs, stores, at = [], [], [], 0
    for nv, ns in PR["END"]:
        names = []
        for n, pcs, nm in ((nv, vpcs, "qv%d"), (ns, spcs, "qs%d")):
            if n:
                names.append(nm % len(pcs))
                pcs.append((at, at + n))
                at += n
        stores.append((names, at - nv - ns, at))
    ADD = S - at

    def far_first(r):
        rest = [x for x in range(N) if x != r]
        return sorted(rest, key=lambda x: (topo.die(T.cores[x]) == topo.die(T.cores[r]), x ^ r))

    others = far_first(q)
    order = others + [q]
    eng = topo.engines(core, T.cores[others[0]])

    def blk(r, lo=0, hi=CAP):
        return slice(r * CAP + lo, r * CAP + hi)

    def lst(r, lo=0, hi=CAP):
        return T.invu[:, r * KB + lo // 16:r * KB + hi // 16]

    def dst(r):
        rid, pid, _ = topo.addr(T.cores[r])
        return DstId(rid=rid, pnc=pid)

    def wait(e, *names):
        for nm in names:
            nm, k = nm if isinstance(nm, tuple) else (nm, 1)
            e.wait_ge(sem[nm], k)

    def ps(k):
        return T["ps%d" % k]

    for k in range(NA):
        sy.dma_start(T.xs[:, ACUT[k]:ACUT[k + 1]], T.a[:, ACUT[k]:ACUT[k + 1]]).then_inc(sem["la%d" % k], 16)
    lsa, lsb, sai = "lsa", "lsb", T.sau
    sy.dma_start(T.sai[:], T.sa[:]).then_inc(sem.ldsa, 16)
    sy.dma_start(T.sbi[:], T.sb[:]).then_inc(sem.ldsb, 16)
    wait(sy, "zt")
    sy.dma_start(T.inv[0:128:16, :], T.zt[:]).then_inc(sem.ifl, 16)
    sy.dma_start(T.bv[:], T.b[:]).then_inc(sem.ldb, 16)
    sy.dma_start(T.av[:], T.a[:]).then_inc(sem.lda, 16)
    wait(sy, "inv")
    for r in order:
        sy.dma_start(T.tab[:, r * KB:(r + 1) * KB], T.inv[0:128:16, blk(r)]).then_inc(sem.tab, 16)

    g.iota(T.cst[:, CV:S], [[0, S - CV]], -15, 0, allow_small_or_imprecise_dtypes=True).then_inc(sem.z2, 1)
    g.iota(T.xs[:, S:W], [[0, W - S]], 0, 0, allow_small_or_imprecise_dtypes=True).then_inc(sem.zxs, 1)
    for k in range(2):
        g.iota(T.plc[:, k * HS:(k + 1) * HS], [[1, HS]], OFS + k * HS, 0,
               allow_small_or_imprecise_dtypes=True).then_inc(sem["iot%d" % k], 1)
    wait(g, "ones")
    g.affine_select(T.idp[:], T.onp[:], [[-1, 128]], A.is_equal, 0.0, 0, 1).then_inc(sem.idp, 1)

    v.memset(T.cst[:, 0:K], -15.0).then_inc(sem.z0, 1)
    v.memset(T.cst[:, K:CV], -15.0).then_inc(sem.z1, 1)
    v.memset(T.fx[:, 0:1], -15.0).then_inc(sem.zx0, 1)
    v.memset(T.bw[:, S + 15:S + 16], -15.0).then_inc(sem.zb, 1)
    v.memset(T.onp[:], 1.0).then_inc(sem.ones, 1)
    wait(v, "z0", "z1")
    for k in range(NA):
        lo, hi = ACUT[k], ACUT[k + 1]
        wait(v, ("la%d" % k, 16))
        if k:
            wait(v, "fa%d" % (k - 1))
        out = T.fx if k < NA - 1 else T.fw
        v.tensor_tensor_scan(out[:, lo + 1:hi + 1], T.xs[:, lo:hi], T.cst[:, 0:hi - lo], T.fx[:, lo:lo + 1] if k else -15.0,
                             A.add, A.max).then_inc(sem["fa%d" % k], 1)
    wait(v, "z2")
    v.tensor_tensor_scan(T.bw[:, S + 14:14:-1], T.xs[:, S - 1::-1], T.cst[:], -15.0, A.add, A.max).then_inc(sem.b1, 1)
    wait(v, ("ldsa", 16))
    v.tensor_copy(T.sau[:], T.sai[:]).then_inc(sem.lsa, 1)
    wait(v, ("ldsb", 16))
    v.tensor_copy(T.sbu[:], T.sbi[:]).then_inc(sem.lsb, 1)
    wait(v, "b1", lsa, "zxs")
    for k in range(NX):
        lo, hi = XCUT[k], XCUT[k + 1]
        wait(v, "bc%d" % k, *["fc%d" % j for j in range(NA) if ACUT[j] < hi])
        if k:
            wait(v, "x%d" % (k - 1))
        else:
            wait(v, "fa%d" % (NA - 1))
        v.tensor_tensor(T.xs[:, 0:W].indirect(T.sau[:, lo // 16:hi // 16]), T.fc[:, lo:hi], T.bc[:, lo:hi],
                        A.add).then_inc(sem["x%d" % k], 1)
    xlast = "x%d" % (NX - 1)

    wait(s, "z0")
    s.activation(T.zt[:], T.cst[:, 0:K], AF.Silu).then_inc(sem.zt, 1)
    wait(s, "zx0")
    for k in range(NA):
        lo, hi = (ACUT[k] + 1 if k else 0), min(ACUT[k + 1] + 1, S)
        wait(s, "fa%d" % k)
        src = T.fx if k < NA - 1 else T.fw
        s.activation(T.fc[:, lo:hi], src[:, lo:hi], AF.Relu, scale=-1.0).then_inc(sem["fc%d" % k], 1)
    wait(s, "zb", "b1")
    for k in range(NX):
        lo, hi = XCUT[k], XCUT[k + 1]
        s.activation(T.bc[:, lo:hi], T.bw[:, lo + 16:hi + 16], AF.Relu, scale=-1.0).then_inc(sem["bc%d" % k], 1)
    wait(s, ("ifl", 16), "iot0", lsb)
    s.activation(T.inv[:, 0:W].indirect(T.sbu[:, 0:KS // 2]), T.plc[:, 0:HS], AF.Silu).then_inc(sem.inv0, 1)
    wait(s, "inv0", "iot1")
    s.activation(T.inv[:, 0:W].indirect(T.sbu[:, KS // 2:KS]), T.plc[:, HS:S], AF.Silu).then_inc(sem.inv, 1)

    ev, od = eng[0::2], eng[1::2]
    h = len(ev) // 2
    FA = PR["FA"]
    calls = {"b": [[(0, 0, CAP, ev), (1, 0, CAP, od)], [(2, 0, CAP, eng)]],
             "d": [[(0, 0, CAP, ev[:h]), (1, 0, CAP, ev[h:])], [(2, 0, CAP, od)]],
             "h": [[(0, 0, FA, ev[:h]), (1, 0, FA, ev[h:])], [(2, 0, CAP, od)],
                   [(0, FA, CAP, od[:h]), (1, FA, CAP, od[h:])]]}[PR["C1"]]
    wait(g, xlast)
    for c in calls:
        g.remote_dma_fused([RemoteDMATransfer(
            dst_ids=[dst(others[k])], dma_engine_mask=sum(1 << e for e in p), remote_sem=sem.arr1,
            srcs=[T.xs[:, blk(others[k], lo, hi)]], dsts=[T.ys[:, blk(q, lo, hi)]], alu_op=0) for k, lo, hi, p in c],
            local_sem=sem.loc1)
    n1 = narr = sum(len(p) for c in calls for _, _, _, p in c)
    if ADD:
        g.dma_start(T.y[:, S - ADD:S], T.a[:, S - ADD:S]).then_inc(sem.pre, 16)
    wait(v, xlast)
    v.tensor_copy(T.ys[:, blk(q)], T.xs[:, blk(q)]).then_inc(sem.own1, 1)
    v.memset(T.fw[:, 0:1], -15.0).then_inc(sem.zf, 1)
    wait(v, "idp")
    for w, c in ((T.idm, -1.0), (T.wu, -float(CAP)), (T.wq, CAP - 16.0), (T.wo, 16.0)):
        v.tensor_scalar(w[:], T.idp[:], c, None, A.mult).then_inc(sem.wts, 1)
    v.tensor_copy(T.saf[:], sai[:]).then_inc(sem.parts, 1)
    v.tensor_scalar(T.uq[:, 0:KS], sai[:], 1.0 / KB, RND + 0.5 / KB - 0.5, A.mult, A.add).then_inc(sem.parts, 1)
    v.tensor_scalar(T.uq[:, KS:2 * KS], sai[:], 1.0 / CAP, RND + 0.5 / CAP - 0.5, A.mult, A.add).then_inc(sem.parts, 1)
    wait(v, ("ldb", 16))
    v.tensor_scalar(T.bq[:, 0:VS], T.bv[:, 0:VS], 15.0, None, A.add).then_inc(sem.bq, 1)
    wait(v, "pm")
    v.tensor_scalar(T.sam[:], ps(3)[:, 0:KS], RND * 15.0, None, A.add).then_inc(sem.sam, 1)

    wait(te, ("wts", 4), ("ldb", 16))
    for k in range(NS):
        te.matmul(ps(k)[:, 0:CS], T.idm[:], T.bv[:, VS + k * CS:VS + (k + 1) * CS], True, False)
    wait(te, ("parts", 3))
    te.matmul(ps(3)[:, 0:KS], T.wo[:], T.saf[:], True, False)
    te.matmul(ps(3)[:, 0:KS], T.wu[:], T.uq[:, 0:KS], False, False)
    te.matmul(ps(3)[:, 0:KS], T.idp[:], T.uq[:, 0:KS], False, False)
    te.matmul(ps(3)[:, 0:KS], T.wq[:], T.uq[:, KS:2 * KS], False, True).then_inc(sem.pm, 1)
    for k in range(NS):
        wait(te, "gs%d" % k)
        te.matmul(ps(k)[:, 0:CS], T.idp[:], T.gs[:, k * CS:(k + 1) * CS], False, True).then_inc(sem["pl%d" % k], 1)
    wait(te, ("lda", 16))
    for k, (lo, hi) in enumerate(spcs):
        te.matmul(ps(4 + k)[:, 0:hi - lo], T.idp[:], T.av[:, lo:hi], True, False)

    wait(v, "bq")
    for e in (v, s):
        wait(e, lsb, "own1", ("arr1", narr))
    v.tensor_tensor(T.ln[:, 0:VS], T.ys[:, 0:W].indirect(T.sbu[:, 0:VS // 16]), T.bq[:, 0:VS], A.subtract).then_inc(sem.ln, 1)
    for k in range(NS):
        lo = VS + k * CS
        s.activation(T.gs[:, k * CS:(k + 1) * CS], T.ys[:, 0:W].indirect(T.sbu[:, lo // 16:(lo + CS) // 16]),
                     AF.Identity).then_inc(sem["gs%d" % k], 1)
    for k in range(NS):
        lo = VS + k * CS
        wait(s, "pl%d" % k)
        s.activation(T.ln[:, lo:lo + CS], ps(k)[:, 0:CS], AF.Identity, bias=-15.0).then_inc(sem["lc%d" % k], 1)
    if not PR["LATE"]:
        wait(v, ("tab", 16 * N))
        v.tensor_scalar(T.invu[:], T.tab[:], 0.25 - OFS, None, A.add).then_inc(sem.invu, 1)
    wait(v, "ln", *["lc%d" % k for k in range(NS)])
    v.tensor_tensor_scan(T.fw[:, 1:S + 1], T.ln[:], T.cst[:], -15.0, A.add, A.min).then_inc(sem.f2, 1)
    if PR["LATE"]:
        wait(v, ("tab", 16 * N))
        v.tensor_scalar(T.invu[:], T.tab[:], 0.25 - OFS, None, A.add).then_inc(sem.invu, 1)
    v.tensor_tensor_scan(T.bw[:, S + 14:14:-1], T.ln[:, ::-1], T.cst[:], -15.0, A.add, A.min).then_inc(sem.b2, 1)

    fwin, bwin = T.fw[:, 0:S], T.bw[:, 16:S + 16]
    wait(s, "invu", "zf", "zb", "f2")
    wait(v, "invu", "zb", "b2")
    wait(te, "sam", *["lc%d" % k for k in range(NS)])
    units = PR["UNITS"]
    banks = [0, 1, 2, 3, 6, 7]
    ahead, at, cnt = [], 0, [0] * len(units)
    for b, lo, hi, vb, how in units:
        ahead.append(min(hi, lo + max(0, PR["AHEAD"] - at)))
        at += hi - lo

    def sget(kind, k, lo, hi):
        if lo < hi:
            r = order[units[k][0]]
            out, win = (T.gf, fwin) if kind == "F" else (T.gb, bwin)
            s.activation(out[:, blk(r, lo, hi)], win.indirect(lst(r, lo, hi)), AF.Relu, bias=30.0).then_inc(sem["sg%d" % k], 1)
            cnt[k] += 1

    def send(k):
        b, lo, hi, vb, how = units[k]
        r = order[b]
        srcs = [T.gf, T.gb] if how == "fold" else [T.ze]
        g.remote_dma_fused([RemoteDMATransfer(
            dst_ids=[dst(r)], dma_engine_mask=topo.mask(core, T.cores[r]), remote_sem=sem["ar%d" % k],
            srcs=[t[:, blk(r, lo, hi)] for t in srcs], dsts=[T.y2[:, blk(q, lo, hi)]], alu_op=len(srcs) - 1)],
            local_sem=sem.loc2)

    def copy_out(k):
        b, lo, hi, vb, how = units[k]
        out = (T.y2 if b == 3 else T.ze)[:, blk(order[b], lo, hi)]
        src = ps(bank[k])[:, 0:hi - lo]
        if how == "s":
            wait(s, "po%d" % k)
            s.activation(out, src, AF.Identity, bias=15.0).then_inc(sem["ze%d" % k], 1)
        else:
            wait(v, "po%d" % k)
            v.tensor_scalar(out, src, 15.0, None, A.add).then_inc(sem["ze%d" % k], 1)
        if b < 3:
            wait(g, "ze%d" % k)
            send(k)

    for k, u in enumerate(units):
        sget("F", k, u[1], ahead[k])
    wait(s, "b2")
    bank, due = {}, []
    for k, (b, lo, hi, vb, how) in enumerate(units):
        r = order[b]
        sget("F", k, ahead[k], hi)
        sget("B", k, vb, hi)
        v.tensor_scalar(T.gb[:, blk(r, lo, vb)], bwin.indirect(lst(r, lo, vb)), -30.0, 30.0,
                        A.max, A.add).then_inc(sem["vg%d" % k], 1)
        for j in due:
            copy_out(j)
        due = []
        if how == "fold":
            wait(g, ("sg%d" % k, cnt[k]), "vg%d" % k)
            send(k)
        else:
            bank[k] = banks.pop(0)
            wait(te, ("sg%d" % k, cnt[k]), "vg%d" % k)
            te.matmul(ps(bank[k])[:, 0:hi - lo], T.idm[:], T.gf[:, blk(r, lo, hi)], True, False)
            te.matmul(ps(bank[k])[:, 0:hi - lo], T.idm[:], T.gb[:, blk(r, lo, hi)], False, True).then_inc(sem["po%d" % k], 1)
            due.append(k)
    for j in due:
        copy_out(j)
    n2 = len(eng) * sum(u[0] < 3 for u in units)
    ready = []
    for k, (b, lo, hi, vb, how) in enumerate(units):
        if b == 3:
            ready.append("ze%d" % k)
        elif how == "fold":
            part = T.y2[:, blk([x for x in others if far_first(x)[b] == q][0], lo, hi)]
            wait(v, ("ar%d" % k, len(eng)))
            v.tensor_scalar(part, part, -1.0, 15.0, A.mult, A.add).then_inc(sem["tn%d" % k], 1)
            ready.append("tn%d" % k)
        else:
            ready.append(("ar%d" % k, len(eng)))

    wait(v, ("lda", 16))
    for e in (v, s):
        wait(e, "sam", *ready)
    ywin = T.y2[:, 0:W]

    def vgather(k):
        lo, hi = vpcs[k]
        v.tensor_tensor(T.qv[:, lo:hi], ywin.indirect(T.sam[:, lo // 16:hi // 16]), T.av[:, lo:hi],
                        A.add).then_inc(sem["qv%d" % k], 1)

    def sgather(k):
        lo, hi = spcs[k]
        s.activation(T.vt[:, lo:hi], ywin.indirect(T.sam[:, lo // 16:hi // 16]), AF.Identity).then_inc(sem["ge%d" % k], 1)
        wait(te, "ge%d" % k)
        te.matmul(ps(4 + k)[:, 0:hi - lo], T.idp[:], T.vt[:, lo:hi], False, True).then_inc(sem["pq%d" % k], 1)

    def scopy(k):
        lo, hi = spcs[k]
        wait(s, "pq%d" % k)
        s.activation(T.qv[:, lo:hi], ps(4 + k)[:, 0:hi - lo], AF.Identity).then_inc(sem["qs%d" % k], 1)

    if ADD:
        s.activation(T.vt[:, S - ADD:S], ywin.indirect(T.sam[:, (S - ADD) // 16:KS]), AF.Identity).then_inc(sem.gadd, 1)
        wait(g, "gadd", ("pre", 16))
        g.dma_start(T.y[:, S - ADD:S], T.vt[:, S - ADD:S], accum_op=A.add).then_inc(sem.pre, 16)
        wait(g, ("pre", 32))
    for k in range(len(vpcs)):
        vgather(k)
    lag = PR["LAG"]
    for j in range(len(spcs) + lag):
        if j < len(spcs):
            sgather(j)
        if j >= lag:
            scopy(j - lag)

    for j, (names, lo, hi) in enumerate(stores):
        e = s if PR["LASTQ"] and j == len(stores) - 1 else sy
        wait(e, *names)
        e.dma_start(T.y[:, lo:hi], T.qv[:, lo:hi]).then_inc(sem.acc, 16)
    wait(g, ("loc1", n1), ("loc2", n2))
    wait(sy, ("acc", 16 * len(stores)))
